import numpy as np
import ml_dtypes


def mxq(x, axis, fmt="e4m3"):
    dtype, down = {"e4m3": (ml_dtypes.float8_e4m3fn, 7), "e5m2": (ml_dtypes.float8_e5m2, 14)}[fmt]
    v = np.moveaxis(np.asarray(x, np.float32).astype(ml_dtypes.bfloat16).astype(np.float64), axis, -1)
    blocks = v.reshape(v.shape[:-1] + (-1, 32))
    amax = np.abs(blocks).max(-1, keepdims=True)
    byte = np.maximum(np.where(amax > 0, np.frexp(amax)[1] - 1 + 127, 0) - down, 1)
    scale = np.exp2(byte - 127.0)
    codes = (blocks / scale).astype(np.float32).astype(dtype).astype(np.float64)
    return np.moveaxis((codes * scale).reshape(v.shape), -1, axis)


WIDE = False


def mx_kscale(k):
    if not WIDE:
        return np.ones(k)
    levels = np.array([10, -10, 5, -5, 0])
    if k % 512:
        return np.exp2(np.random.permutation(np.resize(levels, k // 32))).repeat(32)
    a = np.empty((k // 512, 16))
    for p in range(k // 512):
        a[p, :8] = np.random.permutation(np.resize(levels, 8))
        for g in range(8):
            far = levels[np.abs(levels - a[p, g]) >= 10]
            a[p, g + 8] = far[np.random.randint(len(far))]
    return np.exp2(a.ravel()).repeat(32)


def f64(x):
    return np.asarray(x).astype(np.float64)


def striped(idx):
    return np.tile(idx.reshape(-1, 16).T, (8, 1)).astype(np.uint16)


def unstriped(offs):
    return offs[:16].T.reshape(-1).astype(np.int64)


def pack_weight(w):
    k, n = w.shape
    w = f64(np.asarray(w, np.float32).astype(ml_dtypes.bfloat16)).reshape(k // 32, 32, n)
    amax = np.abs(w).max(1)
    byte = np.clip(np.where(amax > 0, np.frexp(amax)[1] - 1 + 127 - 7, 1), 1, 254)
    scaled = (w * np.exp2(127.0 - byte)[:, None, :]).reshape(k, n).astype(np.float32)
    words = np.ascontiguousarray(scaled.reshape(k // 512, 128, 4, n).transpose(0, 1, 3, 2)).astype(ml_dtypes.float8_e4m3fn).view(np.uint8)
    return words, np.ascontiguousarray(byte.astype(np.uint8).reshape(k // 512, 16, n))


def unpack_weight(words, scales):
    g, p, n, _ = words.shape
    vals = np.ascontiguousarray(words).view(ml_dtypes.float8_e4m3fn).astype(np.float64) * np.repeat(np.exp2(scales.astype(np.float64) - 127.0), 8, axis=1)[..., None]
    return vals.transpose(0, 1, 3, 2).reshape(g * 512, n)


K, T, S, N, H = 1024, 1024, 512, 128, 512


def setup_inputs():
    n = np.random.standard_normal
    s = mx_kscale(K)[:, None]
    u = mx_kscale(H)
    packed_xT = pack_weight(n((K, T)) * s)
    return {
        "x_words": packed_xT[0],
        "x_scales": packed_xT[1],
        "w1": (n((K, H)) / np.sqrt(K) / s).astype(np.float32),
        "prior": (0.5 * n((H, S))).astype(np.float32),
        "invn": (np.random.uniform(0.7, 1.5, (H, 1))).astype(np.float32),
        "unit": (np.random.uniform(0.5, 1.5, (H, 1)) * u[:, None]).astype(np.float32),
        "code": (n((H, N)) / np.sqrt(H) / u[:, None]).astype(np.float32),
        "rx": (1.3 * n((N, S))).astype(np.float32),
        "offs": striped(np.random.permutation(T)[:S]),
    }


def reference(x_words, x_scales, w1, prior, invn, unit, code, rx, offs):
    xq = unpack_weight(x_words, x_scales)[:, unstriped(offs)]
    y = mxq(f64(w1), 0, "e4m3").T @ xq
    llr = 1.2 * (f64(invn) * y) + f64(prior)
    sym = np.tanh(0.5 * llr)
    amp = f64(unit) * sym
    rec = mxq(f64(code), 0, "e4m3").T @ mxq(amp, 0, "e4m3")
    return f64(rx) - rec

@@ -1,0 +1,149 @@
+from contextlib import ExitStack
+
+import concourse.mybir as mybir
+
+K, T, S, N, H = 1024, 1024, 512, 128, 512
+FLOPS = 2 * K * H * S + 2 * H * N * S
+
+F32 = mybir.dt.float32
+BF16 = mybir.dt.bfloat16
+I32 = mybir.dt.int32
+U32 = mybir.dt.uint32
+U16 = mybir.dt.uint16
+U8 = mybir.dt.uint8
+FP8X4 = mybir.dt.float8_e4m3fn_x4
+ALU = mybir.AluOpType
+ACT = mybir.ActivationFunctionType
+
+P = 128
+PACK = 4
+PASSES = K // (P * PACK)
+HALVES = 2
+HALF = S // HALVES
+VECTOR_M = 84
+
+
+def tile_picked_ysicst_res_p_kernel(
+    tc, x_words, x_scales, w1, prior, invn, unit, code, rx, offs, out
+):
+    nc = tc.nc
+    with ExitStack() as ctx:
+        keep = ctx.enter_context(tc.tile_pool(name="keep", bufs=1))
+        psum = ctx.enter_context(tc.psum_pool(name="psum", bufs=1))
+
+        offsets = keep.tile([P, S // 16], U16, name="offsets")
+        words = [keep.tile([P, T], U32, name="words%d" % g) for g in range(PASSES)]
+        planes = keep.tile([P, T], U8, name="planes")
+        w_raw = [keep.tile([P, PACK, H], F32, name="w_raw%d" % g) for g in range(PASSES)]
+        prior_sb = [keep.tile([P, PACK, HALF], F32, name="prior%d" % h) for h in range(HALVES)]
+        code_raw = keep.tile([P, PACK, N], F32, name="code_raw")
+        rx_sb = keep.tile([P, S], F32, name="rx_sb")
+        invn_sb = keep.tile([P, PACK], F32, name="invn_sb")
+        unit_sb = keep.tile([P, PACK], F32, name="unit_sb")
+        gain = keep.tile([P, PACK], F32, name="gain")
+        warm_in = keep.tile([P, 1], F32, name="warm_in")
+        warm_out = keep.tile([P, 1], F32, name="warm_out")
+
+        nc.vector.memset(warm_in[:], 0.0)
+        nc.scalar.activation(warm_out[:], warm_in[:], ACT.Tanh)
+
+        nc.gpsimd.memset(planes[:].bitcast(I32), 0)
+        for q in range(4):
+            nc.gpsimd.dma_start(
+                out=planes[32 * q : 32 * q + 4 * PASSES, :].bitcast(I32),
+                in_=x_scales[:, 4 * q : 4 * q + 4, :].bitcast(I32),
+            )
+        nc.gpsimd.dma_start(out=invn_sb[:], in_=invn.rearrange("(p t) o -> p (t o)", t=PACK))
+        nc.gpsimd.dma_start(out=unit_sb[:], in_=unit.rearrange("(p t) o -> p (t o)", t=PACK))
+
+        nc.sync.dma_start(out=words[0][:].bitcast(I32), in_=x_words[0].rearrange("p n t -> p (n t)").bitcast(I32))
+        nc.sync.dma_start(offsets[:], offs)
+        w_rows = w1.rearrange("(g p j) c -> g p j c", g=PASSES, j=PACK)
+        nc.sync.dma_start(out=w_raw[0][:], in_=w_rows[0])
+        nc.sync.dma_start(out=words[1][:].bitcast(I32), in_=x_words[1].rearrange("p n t -> p (n t)").bitcast(I32))
+        nc.sync.dma_start(out=w_raw[1][:], in_=w_rows[1])
+        prior_rows = prior.rearrange("(p t) s -> p t s", t=PACK)
+        nc.sync.dma_start(out=prior_sb[0][:], in_=prior_rows[:, :, 0:HALF])
+        nc.sync.dma_start(out=prior_sb[1][:], in_=prior_rows[:, :, HALF:S])
+        nc.sync.dma_start(out=code_raw[:], in_=code.rearrange("(p j) n -> p j n", j=PACK))
+        nc.sync.dma_start(out=rx_sb[:], in_=rx)
+
+        x_codes = [keep.tile([P, S], U32, name="x_codes%d" % g, align_bytes=64) for g in range(PASSES)]
+        x_planes = keep.tile([P, S], U8, name="x_planes", align_bytes=64)
+        nc.vector.tensor_copy(x_codes[0][:], words[0][:].indirect(offsets[:]))
+        nc.vector.tensor_copy(x_planes[:], planes[:].indirect(offsets[:]))
+        nc.gpsimd.tensor_scalar(gain[:], invn_sb[:], 1.2, 1.0, ALU.mult, ALU.mult)
+
+        y = [[psum.tile([P, HALF], F32, name="y%d_%d" % (h, t), tag="bank%d_%d" % (h, t)) for t in range(PACK)] for h in range(HALVES)]
+
+        for g in range(PASSES):
+            grouped = keep.tile([P, PACK, P, PACK], BF16, name="w_grouped%d" % g, align_bytes=64)
+            src = w_raw[g][:].rearrange("p j (m t) -> p m t j", t=PACK)
+            dst = grouped[:].rearrange("p t m j -> p m t j")
+            nc.vector.tensor_copy(dst[:, 0:VECTOR_M], src[:, 0:VECTOR_M])
+            nc.scalar.copy(dst[:, VECTOR_M:P], src[:, VECTOR_M:P])
+            w_codes = [keep.tile([P, P], U32, name="w_codes%d_%d" % (g, t), align_bytes=64) for t in range(PACK)]
+            w_planes = [keep.tile([P, P], U8, name="w_planes%d_%d" % (g, t), align_bytes=64) for t in range(PACK)]
+            for t in range(PACK):
+                nc.vector.quantize_mx(
+                    out=w_codes[t][:].bitcast(FP8X4),
+                    scales=w_planes[t][:],
+                    in_=grouped[:, t].rearrange("p m j -> p (m j)"),
+                )
+            if g == 0:
+                nc.vector.tensor_copy(x_codes[1][:], words[1][:].indirect(offsets[:]))
+            for h in range(HALVES):
+                cols = slice(h * HALF, (h + 1) * HALF)
+                for t in range(PACK):
+                    nc.tensor.matmul_mx(
+                        out=y[h][t][:],
+                        lhsT=w_codes[t][:].bitcast(FP8X4),
+                        lhsT_scale=w_planes[t][:],
+                        rhs=x_codes[g][:, cols].bitcast(FP8X4),
+                        rhs_scale=x_planes[4 * g : P, cols],
+                        start=(g == 0),
+                        stop=(g == PASSES - 1),
+                    )
+
+        llr = [[keep.tile([P, HALF], F32, name="llr%d_%d" % (h, t)) for t in range(PACK)] for h in range(HALVES)]
+        sym = [[keep.tile([P, HALF], F32, name="sym%d_%d" % (h, t)) for t in range(PACK)] for h in range(HALVES)]
+        amp = [keep.tile([P, PACK, HALF], BF16, name="amp%d" % h) for h in range(HALVES)]
+        for h in range(HALVES):
+            for t in range(PACK):
+                nc.vector.scalar_tensor_tensor(
+                    llr[h][t][:], y[h][t][:], gain[:, t : t + 1], prior_sb[h][:, t, :], ALU.mult, ALU.add
+                )
+                nc.scalar.activation(sym[h][t][:], llr[h][t][:], ACT.Tanh, scale=0.5)
+                nc.gpsimd.tensor_scalar(amp[h][:, t, :], sym[h][t][:], unit_sb[:, t : t + 1], 1.0, ALU.mult, ALU.mult)
+
+        code_grouped = keep.tile([P, N, PACK], BF16, name="code_grouped", align_bytes=64)
+        nc.scalar.copy(code_grouped[:], code_raw[:].rearrange("p j n -> p n j"))
+        c_codes = keep.tile([P, N], U32, name="c_codes", align_bytes=64)
+        c_planes = keep.tile([P, N], U8, name="c_planes", align_bytes=64)
+        nc.vector.quantize_mx(
+            out=c_codes[:].bitcast(FP8X4), scales=c_planes[:], in_=code_grouped[:].rearrange("p n j -> p (n j)")
+        )
+
+        chunks = [(0, 0, HALF, nc.vector.tensor_copy), (1, 0, HALF // 2, nc.vector.tensor_copy), (1, HALF // 2, HALF // 2, nc.scalar.copy)]
+        for c, (h, first, width, weave) in enumerate(chunks):
+            cols = slice(h * HALF + first, h * HALF + first + width)
+            amp_grouped = keep.tile([P, width, PACK], BF16, name="amp_grouped%d" % c, align_bytes=64)
+            weave(amp_grouped[:], amp[h][:, :, first : first + width].rearrange("p t s -> p s t"))
+            a_codes = keep.tile([P, width], U32, name="a_codes%d" % c, align_bytes=64)
+            a_planes = keep.tile([P, width], U8, name="a_planes%d" % c, align_bytes=64)
+            nc.vector.quantize_mx(
+                out=a_codes[:].bitcast(FP8X4), scales=a_planes[:], in_=amp_grouped[:].rearrange("p s t -> p (s t)")
+            )
+            rec = psum.tile([P, width], F32, name="rec%d" % c, tag="bank0_%d" % c)
+            nc.tensor.matmul_mx(
+                out=rec[:],
+                lhsT=c_codes[:].bitcast(FP8X4),
+                lhsT_scale=c_planes[:],
+                rhs=a_codes[:].bitcast(FP8X4),
+                rhs_scale=a_planes[:],
+                start=True,
+                stop=True,
+            )
+            result = keep.tile([P, width], F32, name="result%d" % c)
+            nc.vector.tensor_tensor(result[:], rx_sb[:, cols], rec[:], ALU.subtract)
+            nc.sync.dma_start(out=out[:, cols], in_=result[:])

@@ -20,7 +20,7 @@ PACK = 4
 PASSES = K // (P * PACK)
 HALVES = 2
 HALF = S // HALVES
-VECTOR_M = 84
+QUARTER = HALF // 2
 
 
 def tile_picked_ysicst_res_p_kernel(
@@ -34,7 +34,7 @@ def tile_picked_ysicst_res_p_kernel(
         offsets = keep.tile([P, S // 16], U16, name="offsets")
         words = [keep.tile([P, T], U32, name="words%d" % g) for g in range(PASSES)]
         planes = keep.tile([P, T], U8, name="planes")
-        w_raw = [keep.tile([P, PACK, H], F32, name="w_raw%d" % g) for g in range(PASSES)]
+        w_raw = [keep.tile([P, PACK, width], F32, name="w_raw%d" % g) for g, width in enumerate((H, H // 2, H // 2))]
         prior_sb = [keep.tile([P, PACK, HALF], F32, name="prior%d" % h) for h in range(HALVES)]
         code_raw = keep.tile([P, PACK, N], F32, name="code_raw")
         rx_sb = keep.tile([P, S], F32, name="rx_sb")
@@ -44,91 +44,121 @@ def tile_picked_ysicst_res_p_kernel(
         warm_in = keep.tile([P, 1], F32, name="warm_in")
         warm_out = keep.tile([P, 1], F32, name="warm_out")
 
+        nc.gpsimd.memset(planes[:].bitcast(I32), 0)
         nc.vector.memset(warm_in[:], 0.0)
         nc.scalar.activation(warm_out[:], warm_in[:], ACT.Tanh)
 
-        nc.gpsimd.memset(planes[:].bitcast(I32), 0)
-        for q in range(4):
-            nc.gpsimd.dma_start(
-                out=planes[32 * q : 32 * q + 4 * PASSES, :].bitcast(I32),
-                in_=x_scales[:, 4 * q : 4 * q + 4, :].bitcast(I32),
-            )
-        nc.gpsimd.dma_start(out=invn_sb[:], in_=invn.rearrange("(p t) o -> p (t o)", t=PACK))
-        nc.gpsimd.dma_start(out=unit_sb[:], in_=unit.rearrange("(p t) o -> p (t o)", t=PACK))
+        def load_words(g):
+            nc.sync.dma_start(out=words[g][:].bitcast(I32), in_=x_words[g].rearrange("p n t -> p (n t)").bitcast(I32))
 
-        nc.sync.dma_start(out=words[0][:].bitcast(I32), in_=x_words[0].rearrange("p n t -> p (n t)").bitcast(I32))
-        nc.sync.dma_start(offsets[:], offs)
+        def load_planes(eng):
+            for q in range(4):
+                eng.dma_start(
+                    out=planes[32 * q : 32 * q + 4 * PASSES, :].bitcast(I32),
+                    in_=x_scales[:, 4 * q : 4 * q + 4, :].bitcast(I32),
+                )
+
         w_rows = w1.rearrange("(g p j) c -> g p j c", g=PASSES, j=PACK)
-        nc.sync.dma_start(out=w_raw[0][:], in_=w_rows[0])
-        nc.sync.dma_start(out=words[1][:].bitcast(I32), in_=x_words[1].rearrange("p n t -> p (n t)").bitcast(I32))
-        nc.sync.dma_start(out=w_raw[1][:], in_=w_rows[1])
         prior_rows = prior.rearrange("(p t) s -> p t s", t=PACK)
-        nc.sync.dma_start(out=prior_sb[0][:], in_=prior_rows[:, :, 0:HALF])
-        nc.sync.dma_start(out=prior_sb[1][:], in_=prior_rows[:, :, HALF:S])
+
+        def load_w(g):
+            if g == 0:
+                nc.sync.dma_start(out=w_raw[0][:], in_=w_rows[0])
+            else:
+                nc.sync.dma_start(out=w_raw[1][:], in_=w_rows[1][:, :, 0 : H // 2])
+                load_small(nc.sync)
+                nc.sync.dma_start(out=w_raw[2][:], in_=w_rows[1][:, :, H // 2 : H])
+
+        def load_small(eng):
+            eng.dma_start(out=invn_sb[:], in_=invn.rearrange("(p t) o -> p (t o)", t=PACK))
+            eng.dma_start(out=unit_sb[:], in_=unit.rearrange("(p t) o -> p (t o)", t=PACK))
+
+        def load_prior(h):
+            nc.sync.dma_start(out=prior_sb[h][:], in_=prior_rows[:, :, h * HALF : (h + 1) * HALF])
+
+        nc.sync.dma_start(offsets[:], offs)
+        load_words(0)
+        load_planes(nc.sync)
+        load_w(0)
+        load_words(1)
+        load_w(1)
         nc.sync.dma_start(out=code_raw[:], in_=code.rearrange("(p j) n -> p j n", j=PACK))
+        load_prior(0)
+        load_prior(1)
         nc.sync.dma_start(out=rx_sb[:], in_=rx)
 
         x_codes = [keep.tile([P, S], U32, name="x_codes%d" % g, align_bytes=64) for g in range(PASSES)]
         x_planes = keep.tile([P, S], U8, name="x_planes", align_bytes=64)
         nc.vector.tensor_copy(x_codes[0][:], words[0][:].indirect(offsets[:]))
         nc.vector.tensor_copy(x_planes[:], planes[:].indirect(offsets[:]))
-        nc.gpsimd.tensor_scalar(gain[:], invn_sb[:], 1.2, 1.0, ALU.mult, ALU.mult)
 
         y = [[psum.tile([P, HALF], F32, name="y%d_%d" % (h, t), tag="bank%d_%d" % (h, t)) for t in range(PACK)] for h in range(HALVES)]
 
-        for g in range(PASSES):
-            grouped = keep.tile([P, PACK, P, PACK], BF16, name="w_grouped%d" % g, align_bytes=64)
-            src = w_raw[g][:].rearrange("p j (m t) -> p m t j", t=PACK)
-            dst = grouped[:].rearrange("p t m j -> p m t j")
-            nc.vector.tensor_copy(dst[:, 0:VECTOR_M], src[:, 0:VECTOR_M])
-            nc.scalar.copy(dst[:, VECTOR_M:P], src[:, VECTOR_M:P])
-            w_codes = [keep.tile([P, P], U32, name="w_codes%d_%d" % (g, t), align_bytes=64) for t in range(PACK)]
-            w_planes = [keep.tile([P, P], U8, name="w_planes%d_%d" % (g, t), align_bytes=64) for t in range(PACK)]
-            for t in range(PACK):
-                nc.vector.quantize_mx(
-                    out=w_codes[t][:].bitcast(FP8X4),
-                    scales=w_planes[t][:],
-                    in_=grouped[:, t].rearrange("p m j -> p (m j)"),
-                )
-            if g == 0:
-                nc.vector.tensor_copy(x_codes[1][:], words[1][:].indirect(offsets[:]))
+        w_codes = [[keep.tile([P, 2 * P], U32, name="w_codes%d_%d" % (g, u), align_bytes=64) for u in range(2)] for g in range(PASSES)]
+        w_planes = [[keep.tile([P, 2 * P], U8, name="w_planes%d_%d" % (g, u), align_bytes=64) for u in range(2)] for g in range(PASSES)]
+
+        def w_piece(g, raw, first, count):
+            for u, cast in enumerate((nc.vector.tensor_copy, nc.scalar.copy)):
+                grouped = keep.tile([P, 2, count, PACK], BF16, name="w_grouped%d_%d_%d" % (g, first, u), align_bytes=64)
+                src = raw[:].rearrange("p j (m t) -> p m t j", t=PACK)[:, :, 2 * u : 2 * u + 2, :]
+                cast(grouped[:].rearrange("p t m j -> p m t j"), src)
+                if count == P:
+                    nc.vector.quantize_mx(
+                        out=w_codes[g][u][:].bitcast(FP8X4),
+                        scales=w_planes[g][u][:],
+                        in_=grouped[:].rearrange("p t m j -> p (t m j)"),
+                    )
+                else:
+                    for e in range(2):
+                        start = e * P + first
+                        nc.vector.quantize_mx(
+                            out=w_codes[g][u][:, start : start + count].bitcast(FP8X4),
+                            scales=w_planes[g][u][:, start : start + count],
+                            in_=grouped[:, e].rearrange("p m j -> p (m j)"),
+                        )
+
+        def products(g):
             for h in range(HALVES):
                 cols = slice(h * HALF, (h + 1) * HALF)
                 for t in range(PACK):
                     nc.tensor.matmul_mx(
                         out=y[h][t][:],
-                        lhsT=w_codes[t][:].bitcast(FP8X4),
-                        lhsT_scale=w_planes[t][:],
+                        lhsT=w_codes[g][t // 2][:, (t % 2) * P : (t % 2 + 1) * P].bitcast(FP8X4),
+                        lhsT_scale=w_planes[g][t // 2][:, (t % 2) * P : (t % 2 + 1) * P],
                         rhs=x_codes[g][:, cols].bitcast(FP8X4),
                         rhs_scale=x_planes[4 * g : P, cols],
                         start=(g == 0),
                         stop=(g == PASSES - 1),
                     )
 
-        llr = [[keep.tile([P, HALF], F32, name="llr%d_%d" % (h, t)) for t in range(PACK)] for h in range(HALVES)]
-        sym = [[keep.tile([P, HALF], F32, name="sym%d_%d" % (h, t)) for t in range(PACK)] for h in range(HALVES)]
-        amp = [keep.tile([P, PACK, HALF], BF16, name="amp%d" % h) for h in range(HALVES)]
-        for h in range(HALVES):
-            for t in range(PACK):
-                nc.vector.scalar_tensor_tensor(
-                    llr[h][t][:], y[h][t][:], gain[:, t : t + 1], prior_sb[h][:, t, :], ALU.mult, ALU.add
-                )
-                nc.scalar.activation(sym[h][t][:], llr[h][t][:], ACT.Tanh, scale=0.5)
-                nc.gpsimd.tensor_scalar(amp[h][:, t, :], sym[h][t][:], unit_sb[:, t : t + 1], 1.0, ALU.mult, ALU.mult)
+        w_piece(0, w_raw[0], 0, P)
+        nc.vector.tensor_copy(x_codes[1][:], words[1][:].indirect(offsets[:]))
+        products(0)
+        w_piece(1, w_raw[1], 0, P // 2)
+        w_piece(1, w_raw[2], P // 2, P // 2)
+        products(1)
+
+        nc.vector.tensor_scalar(gain[:], invn_sb[:], 1.2, None, ALU.mult)
+        llr = [keep.tile([P, PACK, HALF], F32, name="llr%d" % h) for h in range(HALVES)]
+
+        def log_ratio(h, t):
+            nc.vector.scalar_tensor_tensor(
+                llr[h][:, t, :], y[h][t][:], gain[:, t : t + 1], prior_sb[h][:, t, :], ALU.mult, ALU.add
+            )
 
         code_grouped = keep.tile([P, N, PACK], BF16, name="code_grouped", align_bytes=64)
-        nc.scalar.copy(code_grouped[:], code_raw[:].rearrange("p j n -> p n j"))
         c_codes = keep.tile([P, N], U32, name="c_codes", align_bytes=64)
         c_planes = keep.tile([P, N], U8, name="c_planes", align_bytes=64)
-        nc.vector.quantize_mx(
-            out=c_codes[:].bitcast(FP8X4), scales=c_planes[:], in_=code_grouped[:].rearrange("p n j -> p (n j)")
-        )
 
-        chunks = [(0, 0, HALF, nc.vector.tensor_copy), (1, 0, HALF // 2, nc.vector.tensor_copy), (1, HALF // 2, HALF // 2, nc.scalar.copy)]
-        for c, (h, first, width, weave) in enumerate(chunks):
-            cols = slice(h * HALF + first, h * HALF + first + width)
-            amp_grouped = keep.tile([P, width, PACK], BF16, name="amp_grouped%d" % c, align_bytes=64)
-            weave(amp_grouped[:], amp[h][:, :, first : first + width].rearrange("p t s -> p s t"))
+        def code_cast(cast):
+            cast(code_grouped[:], code_raw[:].rearrange("p j n -> p n j"))
+
+        def code_quant():
+            nc.vector.quantize_mx(
+                out=c_codes[:].bitcast(FP8X4), scales=c_planes[:], in_=code_grouped[:].rearrange("p n j -> p (n j)")
+            )
+
+        def quant(c, amp_grouped, width):
             a_codes = keep.tile([P, width], U32, name="a_codes%d" % c, align_bytes=64)
             a_planes = keep.tile([P, width], U8, name="a_planes%d" % c, align_bytes=64)
             nc.vector.quantize_mx(
@@ -144,6 +174,44 @@ def tile_picked_ysicst_res_p_kernel(
                 start=True,
                 stop=True,
             )
+            return rec
+
+        def finish(c, rec, first, width):
+            cols = slice(first, first + width)
             result = keep.tile([P, width], F32, name="result%d" % c)
             nc.vector.tensor_tensor(result[:], rx_sb[:, cols], rec[:], ALU.subtract)
             nc.sync.dma_start(out=out[:, cols], in_=result[:])
+
+        def woven_tanh(c, h, first, width):
+            sym = keep.tile([P, width, PACK], F32, name="symw%d" % c)
+            nc.scalar.activation(sym[:], llr[h][:, :, first : first + width].rearrange("p t s -> p s t"), ACT.Tanh, scale=0.5)
+            return sym
+
+        def woven_mult(c, sym, width):
+            amp_grouped = keep.tile([P, width, PACK], BF16, name="amp_grouped%d" % c, align_bytes=64)
+            nc.vector.tensor_tensor(amp_grouped[:], sym[:], unit_sb[:].unsqueeze(1).to_broadcast([P, width, PACK]), ALU.mult)
+            return amp_grouped
+
+        def weave(c, amp, first, width, copy):
+            amp_grouped = keep.tile([P, width, PACK], BF16, name="amp_grouped%d" % c, align_bytes=64)
+            copy(amp_grouped[:], amp[:, :, first : first + width].rearrange("p t s -> p s t"))
+            return amp_grouped
+
+        code_cast(nc.scalar.copy)
+        code_quant()
+        for h in range(HALVES):
+            for t in range(PACK):
+                log_ratio(h, t)
+        syms = [woven_tanh(c, c // 2, (c % 2) * QUARTER, QUARTER) for c in range(4)]
+        g0 = woven_mult(0, syms[0], QUARTER)
+        g1 = woven_mult(1, syms[1], QUARTER)
+        r0 = quant(0, g0, QUARTER)
+        g2 = woven_mult(2, syms[2], QUARTER)
+        r1 = quant(1, g1, QUARTER)
+        g3 = woven_mult(3, syms[3], QUARTER)
+        r2 = quant(2, g2, QUARTER)
+        finish(0, r0, 0, QUARTER)
+        r3 = quant(3, g3, QUARTER)
+        finish(1, r1, QUARTER, QUARTER)
+        finish(2, r2, 2 * QUARTER, QUARTER)
+        finish(3, r3, 3 * QUARTER, QUARTER)

@@ -35,7 +35,7 @@ def tile_picked_ysicst_res_p_kernel(
         words = [keep.tile([P, T], U32, name="words%d" % g) for g in range(PASSES)]
         planes = keep.tile([P, T], U8, name="planes")
         w_raw = [keep.tile([P, PACK, width], F32, name="w_raw%d" % g) for g, width in enumerate((H, H // 2, H // 2))]
-        prior_sb = [keep.tile([P, PACK, HALF], F32, name="prior%d" % h) for h in range(HALVES)]
+        prior_sb = [[keep.tile([P, 2, HALF], F32, name="prior%d_%d" % (h, u)) for u in range(2)] for h in range(HALVES)]
         code_raw = keep.tile([P, PACK, N], F32, name="code_raw")
         rx_sb = keep.tile([P, S], F32, name="rx_sb")
         invn_sb = keep.tile([P, PACK], F32, name="invn_sb")
@@ -66,7 +66,6 @@ def tile_picked_ysicst_res_p_kernel(
                 nc.sync.dma_start(out=w_raw[0][:], in_=w_rows[0])
             else:
                 nc.sync.dma_start(out=w_raw[1][:], in_=w_rows[1][:, :, 0 : H // 2])
-                load_small(nc.sync)
                 nc.sync.dma_start(out=w_raw[2][:], in_=w_rows[1][:, :, H // 2 : H])
 
         def load_small(eng):
@@ -74,15 +73,17 @@ def tile_picked_ysicst_res_p_kernel(
             eng.dma_start(out=unit_sb[:], in_=unit.rearrange("(p t) o -> p (t o)", t=PACK))
 
         def load_prior(h):
-            nc.sync.dma_start(out=prior_sb[h][:], in_=prior_rows[:, :, h * HALF : (h + 1) * HALF])
+            for u in range(2):
+                nc.sync.dma_start(out=prior_sb[h][u][:], in_=prior_rows[:, 2 * u : 2 * u + 2, h * HALF : (h + 1) * HALF])
 
-        nc.sync.dma_start(offsets[:], offs)
         load_words(0)
+        nc.sync.dma_start(offsets[:], offs)
         load_planes(nc.sync)
         load_w(0)
         load_words(1)
         load_w(1)
         nc.sync.dma_start(out=code_raw[:], in_=code.rearrange("(p j) n -> p j n", j=PACK))
+        load_small(nc.sync)
         load_prior(0)
         load_prior(1)
         nc.sync.dma_start(out=rx_sb[:], in_=rx)
@@ -138,12 +139,12 @@ def tile_picked_ysicst_res_p_kernel(
         w_piece(1, w_raw[2], P // 2, P // 2)
         products(1)
 
-        nc.vector.tensor_scalar(gain[:], invn_sb[:], 1.2, None, ALU.mult)
+        nc.scalar.mul(gain[:], invn_sb[:], 1.2)
         llr = [keep.tile([P, PACK, HALF], F32, name="llr%d" % h) for h in range(HALVES)]
 
         def log_ratio(h, t):
             nc.vector.scalar_tensor_tensor(
-                llr[h][:, t, :], y[h][t][:], gain[:, t : t + 1], prior_sb[h][:, t, :], ALU.mult, ALU.add
+                llr[h][:, t, :], y[h][t][:], gain[:, t : t + 1], prior_sb[h][t // 2][:, t % 2, :], ALU.mult, ALU.add
             )
 
         code_grouped = keep.tile([P, N, PACK], BF16, name="code_grouped", align_bytes=64)

from contextlib import ExitStack

import concourse.mybir as mybir

K, T, S, N, H = 1024, 1024, 512, 128, 512
FLOPS = 2 * K * H * S + 2 * H * N * S

F32 = mybir.dt.float32
BF16 = mybir.dt.bfloat16
I32 = mybir.dt.int32
U32 = mybir.dt.uint32
U16 = mybir.dt.uint16
U8 = mybir.dt.uint8
FP8X4 = mybir.dt.float8_e4m3fn_x4
ALU = mybir.AluOpType
ACT = mybir.ActivationFunctionType

P = 128
PACK = 4
PASSES = K // (P * PACK)
HALVES = 2
HALF = S // HALVES
QUARTER = HALF // 2


def tile_picked_ysicst_res_p_kernel(
    tc, x_words, x_scales, w1, prior, invn, unit, code, rx, offs, out
):
    nc = tc.nc
    with ExitStack() as ctx:
        keep = ctx.enter_context(tc.tile_pool(name="keep", bufs=1))
        psum = ctx.enter_context(tc.psum_pool(name="psum", bufs=1))

        offsets = keep.tile([P, S // 16], U16, name="offsets")
        words = [keep.tile([P, T], U32, name="words%d" % g) for g in range(PASSES)]
        planes = keep.tile([P, T], U8, name="planes")
        w_raw = [keep.tile([P, PACK, width], F32, name="w_raw%d" % g) for g, width in enumerate((H, H // 2, H // 2))]
        prior_sb = [[keep.tile([P, 2, HALF], F32, name="prior%d_%d" % (h, u)) for u in range(2)] for h in range(HALVES)]
        code_raw = keep.tile([P, PACK, N], F32, name="code_raw")
        rx_sb = keep.tile([P, S], F32, name="rx_sb")
        invn_sb = keep.tile([P, PACK], F32, name="invn_sb")
        unit_sb = keep.tile([P, PACK], F32, name="unit_sb")
        gain = keep.tile([P, PACK], F32, name="gain")
        warm_in = keep.tile([P, 1], F32, name="warm_in")
        warm_out = keep.tile([P, 1], F32, name="warm_out")

        nc.gpsimd.memset(planes[:].bitcast(I32), 0)
        nc.vector.memset(warm_in[:], 0.0)
        nc.scalar.activation(warm_out[:], warm_in[:], ACT.Tanh)

        def load_words(g):
            nc.sync.dma_start(out=words[g][:].bitcast(I32), in_=x_words[g].rearrange("p n t -> p (n t)").bitcast(I32))

        def load_planes(eng):
            for q in range(4):
                eng.dma_start(
                    out=planes[32 * q : 32 * q + 4 * PASSES, :].bitcast(I32),
                    in_=x_scales[:, 4 * q : 4 * q + 4, :].bitcast(I32),
                )

        w_rows = w1.rearrange("(g p j) c -> g p j c", g=PASSES, j=PACK)
        prior_rows = prior.rearrange("(p t) s -> p t s", t=PACK)

        def load_w(g):
            if g == 0:
                nc.sync.dma_start(out=w_raw[0][:], in_=w_rows[0])
            else:
                nc.sync.dma_start(out=w_raw[1][:], in_=w_rows[1][:, :, 0 : H // 2])
                nc.sync.dma_start(out=w_raw[2][:], in_=w_rows[1][:, :, H // 2 : H])

        def load_small(eng):
            eng.dma_start(out=invn_sb[:], in_=invn.rearrange("(p t) o -> p (t o)", t=PACK))
            eng.dma_start(out=unit_sb[:], in_=unit.rearrange("(p t) o -> p (t o)", t=PACK))

        def load_prior(h):
            for u in range(2):
                nc.sync.dma_start(out=prior_sb[h][u][:], in_=prior_rows[:, 2 * u : 2 * u + 2, h * HALF : (h + 1) * HALF])

        load_words(0)
        nc.sync.dma_start(offsets[:], offs)
        load_planes(nc.sync)
        load_w(0)
        load_words(1)
        load_w(1)
        nc.sync.dma_start(out=code_raw[:], in_=code.rearrange("(p j) n -> p j n", j=PACK))
        load_small(nc.sync)
        load_prior(0)
        load_prior(1)
        nc.sync.dma_start(out=rx_sb[:], in_=rx)

        x_codes = [keep.tile([P, S], U32, name="x_codes%d" % g, align_bytes=64) for g in range(PASSES)]
        x_planes = keep.tile([P, S], U8, name="x_planes", align_bytes=64)
        nc.vector.tensor_copy(x_codes[0][:], words[0][:].indirect(offsets[:]))
        nc.vector.tensor_copy(x_planes[:], planes[:].indirect(offsets[:]))

        y = [[psum.tile([P, HALF], F32, name="y%d_%d" % (h, t), tag="bank%d_%d" % (h, t)) for t in range(PACK)] for h in range(HALVES)]

        w_codes = [[keep.tile([P, 2 * P], U32, name="w_codes%d_%d" % (g, u), align_bytes=64) for u in range(2)] for g in range(PASSES)]
        w_planes = [[keep.tile([P, 2 * P], U8, name="w_planes%d_%d" % (g, u), align_bytes=64) for u in range(2)] for g in range(PASSES)]

        def w_piece(g, raw, first, count):
            for u, cast in enumerate((nc.vector.tensor_copy, nc.scalar.copy)):
                grouped = keep.tile([P, 2, count, PACK], BF16, name="w_grouped%d_%d_%d" % (g, first, u), align_bytes=64)
                src = raw[:].rearrange("p j (m t) -> p m t j", t=PACK)[:, :, 2 * u : 2 * u + 2, :]
                cast(grouped[:].rearrange("p t m j -> p m t j"), src)
                if count == P:
                    nc.vector.quantize_mx(
                        out=w_codes[g][u][:].bitcast(FP8X4),
                        scales=w_planes[g][u][:],
                        in_=grouped[:].rearrange("p t m j -> p (t m j)"),
                    )
                else:
                    for e in range(2):
                        start = e * P + first
                        nc.vector.quantize_mx(
                            out=w_codes[g][u][:, start : start + count].bitcast(FP8X4),
                            scales=w_planes[g][u][:, start : start + count],
                            in_=grouped[:, e].rearrange("p m j -> p (m j)"),
                        )

        def products(g):
            for h in range(HALVES):
                cols = slice(h * HALF, (h + 1) * HALF)
                for t in range(PACK):
                    nc.tensor.matmul_mx(
                        out=y[h][t][:],
                        lhsT=w_codes[g][t // 2][:, (t % 2) * P : (t % 2 + 1) * P].bitcast(FP8X4),
                        lhsT_scale=w_planes[g][t // 2][:, (t % 2) * P : (t % 2 + 1) * P],
                        rhs=x_codes[g][:, cols].bitcast(FP8X4),
                        rhs_scale=x_planes[4 * g : P, cols],
                        start=(g == 0),
                        stop=(g == PASSES - 1),
                    )

        w_piece(0, w_raw[0], 0, P)
        nc.vector.tensor_copy(x_codes[1][:], words[1][:].indirect(offsets[:]))
        products(0)
        w_piece(1, w_raw[1], 0, P // 2)
        w_piece(1, w_raw[2], P // 2, P // 2)
        products(1)

        nc.scalar.mul(gain[:], invn_sb[:], 1.2)
        llr = [keep.tile([P, PACK, HALF], F32, name="llr%d" % h) for h in range(HALVES)]

        def log_ratio(h, t):
            nc.vector.scalar_tensor_tensor(
                llr[h][:, t, :], y[h][t][:], gain[:, t : t + 1], prior_sb[h][t // 2][:, t % 2, :], ALU.mult, ALU.add
            )

        code_grouped = keep.tile([P, N, PACK], BF16, name="code_grouped", align_bytes=64)
        c_codes = keep.tile([P, N], U32, name="c_codes", align_bytes=64)
        c_planes = keep.tile([P, N], U8, name="c_planes", align_bytes=64)

        def code_cast(cast):
            cast(code_grouped[:], code_raw[:].rearrange("p j n -> p n j"))

        def code_quant():
            nc.vector.quantize_mx(
                out=c_codes[:].bitcast(FP8X4), scales=c_planes[:], in_=code_grouped[:].rearrange("p n j -> p (n j)")
            )

        def quant(c, amp_grouped, width):
            a_codes = keep.tile([P, width], U32, name="a_codes%d" % c, align_bytes=64)
            a_planes = keep.tile([P, width], U8, name="a_planes%d" % c, align_bytes=64)
            nc.vector.quantize_mx(
                out=a_codes[:].bitcast(FP8X4), scales=a_planes[:], in_=amp_grouped[:].rearrange("p s t -> p (s t)")
            )
            rec = psum.tile([P, width], F32, name="rec%d" % c, tag="bank0_%d" % c)
            nc.tensor.matmul_mx(
                out=rec[:],
                lhsT=c_codes[:].bitcast(FP8X4),
                lhsT_scale=c_planes[:],
                rhs=a_codes[:].bitcast(FP8X4),
                rhs_scale=a_planes[:],
                start=True,
                stop=True,
            )
            return rec

        def finish(c, rec, first, width):
            cols = slice(first, first + width)
            result = keep.tile([P, width], F32, name="result%d" % c)
            nc.vector.tensor_tensor(result[:], rx_sb[:, cols], rec[:], ALU.subtract)
            nc.sync.dma_start(out=out[:, cols], in_=result[:])

        def woven_tanh(c, h, first, width):
            sym = keep.tile([P, width, PACK], F32, name="symw%d" % c)
            nc.scalar.activation(sym[:], llr[h][:, :, first : first + width].rearrange("p t s -> p s t"), ACT.Tanh, scale=0.5)
            return sym

        def woven_mult(c, sym, width):
            amp_grouped = keep.tile([P, width, PACK], BF16, name="amp_grouped%d" % c, align_bytes=64)
            nc.vector.tensor_tensor(amp_grouped[:], sym[:], unit_sb[:].unsqueeze(1).to_broadcast([P, width, PACK]), ALU.mult)
            return amp_grouped

        def weave(c, amp, first, width, copy):
            amp_grouped = keep.tile([P, width, PACK], BF16, name="amp_grouped%d" % c, align_bytes=64)
            copy(amp_grouped[:], amp[:, :, first : first + width].rearrange("p t s -> p s t"))
            return amp_grouped

        code_cast(nc.scalar.copy)
        code_quant()
        for h in range(HALVES):
            for t in range(PACK):
                log_ratio(h, t)
        syms = [woven_tanh(c, c // 2, (c % 2) * QUARTER, QUARTER) for c in range(4)]
        g0 = woven_mult(0, syms[0], QUARTER)
        g1 = woven_mult(1, syms[1], QUARTER)
        r0 = quant(0, g0, QUARTER)
        g2 = woven_mult(2, syms[2], QUARTER)
        r1 = quant(1, g1, QUARTER)
        g3 = woven_mult(3, syms[3], QUARTER)
        r2 = quant(2, g2, QUARTER)
        finish(0, r0, 0, QUARTER)
        r3 = quant(3, g3, QUARTER)
        finish(1, r1, QUARTER, QUARTER)
        finish(2, r2, 2 * QUARTER, QUARTER)
        finish(3, r3, 3 * QUARTER, QUARTER)
